import numpy as np
import ml_dtypes


def mxq(x, axis, fmt="e4m3"):
    dtype, down = {"e4m3": (ml_dtypes.float8_e4m3fn, 7), "e5m2": (ml_dtypes.float8_e5m2, 14)}[fmt]
    v = np.moveaxis(np.asarray(x, np.float32).astype(ml_dtypes.bfloat16).astype(np.float64), axis, -1)
    blocks = v.reshape(v.shape[:-1] + (-1, 32))
    amax = np.abs(blocks).max(-1, keepdims=True)
    byte = np.maximum(np.where(amax > 0, np.frexp(amax)[1] - 1 + 127, 0) - down, 1)
    scale = np.exp2(byte - 127.0)
    codes = (blocks / scale).astype(np.float32).astype(dtype).astype(np.float64)
    return np.moveaxis((codes * scale).reshape(v.shape), -1, axis)


WIDE = False


def mx_kscale(k):
    if not WIDE:
        return np.ones(k)
    levels = np.array([30, -30])
    if k % 512:
        return np.exp2(np.random.permutation(np.resize(levels, k // 32))).repeat(32)
    a = np.empty((k // 512, 16))
    for p in range(k // 512):
        a[p, :8] = np.random.permutation(np.resize(levels, 8))
        for g in range(8):
            far = levels[np.abs(levels - a[p, g]) >= 10]
            a[p, g + 8] = far[np.random.randint(len(far))]
    return np.exp2(a.ravel()).repeat(32)


def f64(x):
    return np.asarray(x).astype(np.float64)


def striped(idx):
    return np.tile(np.asarray(idx).reshape(-1, 16).T, (8, 1)).astype(np.uint16)


def unstriped(offs):
    return offs[:16].T.reshape(-1).astype(np.int64)


K, T, J, I, V, G = 1024, 1024, 256, 256, 1024, 32


def setup_inputs():
    n = np.random.standard_normal
    idx = np.random.permutation(T)[:J]
    idx2 = np.random.permutation(T)[:J]
    idx3 = np.random.permutation(V)[:I]
    fk = mx_kscale(K)
    return {
        "xf": (n((K, T)) * 0.03).astype(np.float32),
        "fk": (np.random.uniform(0.5, 2.0, (K, 1)) * fk[:, None]).astype(np.float32),
        "kf": (n((K, V))).astype(np.float32),
        "ko": (n((K, I)) * 0.6).astype(np.float32),
        "fi": (np.random.uniform(0.5, 2.0, (K, 1)) / fk[:, None]).astype(np.float32),
        "bi": (np.random.uniform(-0.7, 0.7, (1, I))).astype(np.float32),
        "offs": striped(idx),
        "offs2": striped(idx2),
        "offs3": striped(idx3),
    }


def reference(xf, fk, kf, ko, fi, bi, offs, offs2, offs3):
    idx = unstriped(offs)
    idx2 = unstriped(offs2)
    idx3 = unstriped(offs3)
    u = (f64(xf)[:, idx] - f64(xf)[:, idx2]) * f64(fk)
    vk = (f64(kf)[:, idx3] + f64(ko)) * f64(fi)
    uq = mxq(u, 0, "e5m2")
    vkq = mxq(vk, 0, "e5m2")
    a0 = uq.T @ vkq
    a = a0 + f64(bi)
    g1 = a.reshape(J, G, I // G).mean(axis=2)
    g2 = np.repeat(g1, I // G, axis=1)
    y = (a - g2) * np.abs(a)
    return y

@@ -1,0 +1,171 @@
+from contextlib import ExitStack
+
+import concourse.mybir as mybir
+from concourse.masks import make_identity
+
+K, T, J, I, V = 1024, 1024, 256, 256, 1024
+BUNDLE = 8
+FLOPS = 2 * K * J * I
+
+F32 = mybir.dt.float32
+BF16 = mybir.dt.bfloat16
+U32 = mybir.dt.uint32
+U16 = mybir.dt.uint16
+U8 = mybir.dt.uint8
+E5M2X4 = mybir.dt.float8_e5m2_x4
+ALU = mybir.AluOpType
+ACT = mybir.ActivationFunctionType
+
+P = 128
+PACK = 4
+PASSES = K // (P * PACK)
+HALF = 128
+HALVES = I // HALF
+ROW_TILES = J // P
+LIST_COLS = J // 16
+
+
+def tile_list_scores_gaps_mixed_centred_f_kernel(tc, xf, fk, kf, ko, fi, bi, offs, offs2, offs3, out):
+    nc = tc.nc
+    xf_v = xf.rearrange("(a p t) c -> a t p c", a=PASSES, t=PACK)
+    kf_v = kf.rearrange("(a p t) c -> a t p c", a=PASSES, t=PACK)
+    ko_v = ko.rearrange("(a p t) c -> a p t c", a=PASSES, t=PACK)
+
+    with ExitStack() as ctx:
+        keep = ctx.enter_context(tc.tile_pool(name="keep", bufs=1))
+        ring = ctx.enter_context(tc.tile_pool(name="ring", bufs=4))
+        psum = ctx.enter_context(tc.psum_pool(name="psum", bufs=1))
+
+        list1 = keep.tile([P, LIST_COLS], U16, name="list1")
+        list2 = keep.tile([P, LIST_COLS], U16, name="list2")
+        list3 = keep.tile([P, LIST_COLS], U16, name="list3")
+        x_pl = [[keep.tile([P, T], F32, name=f"x{a}{t}") for t in range(PACK)] for a in range(PASSES)]
+        k_pl = [[keep.tile([P, V], F32, name=f"k{a}{t}") for t in range(PACK)] for a in range(PASSES)]
+        ko_first = keep.tile([P, PACK, I], F32, name="ko_first")
+        ko_most = keep.tile([P, PACK - 1, I], F32, name="ko_most")
+        ko_last = keep.tile([P, I], F32, name="ko_last")
+        fk_sb = keep.tile([P, PASSES, PACK], F32, name="fk_sb")
+        fi_sb = keep.tile([P, PASSES, PACK], F32, name="fi_sb")
+        bi_pairs = keep.tile([P, 2], F32, name="bi_pairs")
+
+        nc.sync.dma_start(out=x_pl[0][0][:], in_=xf_v[0, 0])
+        nc.sync.dma_start(list2[:], offs2)
+        nc.sync.dma_start(list1[:], offs)
+        for n in range(1, PASSES * PACK):
+            nc.sync.dma_start(out=x_pl[n // PACK][n % PACK][:], in_=xf_v[n // PACK, n % PACK])
+        nc.sync.dma_start(list3[:], offs3)
+        nc.sync.dma_start(out=ko_first[:], in_=ko_v[0])
+        for t in range(PACK):
+            nc.sync.dma_start(out=k_pl[0][t][:], in_=kf_v[0, t])
+        nc.sync.dma_start(out=ko_most[:], in_=ko_v[1, :, 0 : PACK - 1, :])
+        for t in range(PACK):
+            nc.sync.dma_start(out=k_pl[1][t][:], in_=kf_v[1, t])
+        nc.sync.dma_start(out=ko_last[:], in_=ko_v[1, :, PACK - 1, :])
+
+        nc.gpsimd.dma_start(out=fk_sb[:], in_=fk.rearrange("(a p t) o -> p a (t o)", a=PASSES, t=PACK))
+        nc.gpsimd.dma_start(out=fi_sb[:], in_=fi.rearrange("(a p t) o -> p a (t o)", a=PASSES, t=PACK))
+        nc.gpsimd.dma_start(out=bi_pairs[:], in_=bi.rearrange("o (p e) -> p (o e)", e=2))
+
+        ident = keep.tile([P, P], F32, name="ident")
+        make_identity(nc, ident[:])
+        bias_ps = psum.tile([P, 2, P], F32, name="bias_ps")
+        for e in range(2):
+            nc.tensor.transpose(bias_ps[:, e, :], bi_pairs[:, e : e + 1].to_broadcast([P, P]), ident[:])
+        bias = keep.tile([P, I], F32, name="bias")
+
+        u_codes, u_scales = [], []
+        for a in range(PASSES):
+            gaps = keep.tile([P, PACK, J], F32, name=f"gaps{a}")
+            for t in range(PACK):
+                second = ring.tile([P, J], F32, name="second")
+                nc.scalar.activation(second[:], x_pl[a][t][:].indirect(list2[:]), ACT.Copy)
+                nc.vector.tensor_tensor(gaps[:, t, :], x_pl[a][t][:].indirect(list1[:]), second[:], ALU.subtract)
+            u_bf = keep.tile([P, J, PACK], BF16, name=f"u_bf{a}", align_bytes=64)
+            nc.vector.tensor_tensor(
+                u_bf[:].rearrange("p (c i) t -> p c t i", i=4),
+                gaps[:].rearrange("p t (c i) -> p c t i", i=4),
+                fk_sb[:, a, :].unsqueeze(1).unsqueeze(3).broadcast_to([P, J // 4, PACK, 4]),
+                ALU.mult,
+            )
+            codes = keep.tile([P, J], U32, name=f"u_codes{a}", align_bytes=64)
+            scales = keep.tile([P, J], U8, name=f"u_scales{a}", align_bytes=64)
+            nc.vector.quantize_mx(
+                out=codes[:].bitcast(E5M2X4), scales=scales[:], in_=u_bf[:].rearrange("p j t -> p (j t)")
+            )
+            u_codes.append(codes)
+            u_scales.append(scales)
+
+        nc.scalar.copy(bias[:].rearrange("p (n e) -> p n e", e=2), bias_ps[:].rearrange("p e n -> p n e"))
+
+        acc = [psum.tile([P, ROW_TILES, HALF], F32, name=f"acc{h}") for h in range(HALVES)]
+        for a in range(PASSES):
+            v_bf = [keep.tile([P, HALF, PACK], BF16, name=f"v_bf{a}{h}", align_bytes=64) for h in range(HALVES)]
+            for t in range(PACK):
+                if a == 0:
+                    own = ko_first[:, t, :]
+                elif t < PACK - 1:
+                    own = ko_most[:, t, :]
+                else:
+                    own = ko_last[:]
+                sums = []
+                for h in range(HALVES):
+                    picked = ring.tile([P, HALF], F32, name="picked")
+                    part = list3[:, h * (HALF // 16) : (h + 1) * (HALF // 16)]
+                    nc.scalar.activation(picked[:], k_pl[a][t][:].indirect(part), ACT.Copy)
+                    key = ring.tile([P, HALF], F32, name="key")
+                    nc.vector.tensor_tensor(key[:], picked[:], own[:, h * HALF : (h + 1) * HALF], ALU.add)
+                    sums.append(key)
+                for h in range(HALVES):
+                    nc.vector.tensor_scalar(v_bf[h][:, :, t], sums[h][:], fi_sb[:, a, t : t + 1], None, ALU.mult)
+            for h in range(HALVES):
+                codes = keep.tile([P, HALF], U32, name=f"v_codes{a}{h}", align_bytes=64)
+                scales = keep.tile([P, HALF], U8, name=f"v_scales{a}{h}", align_bytes=64)
+                nc.vector.quantize_mx(
+                    out=codes[:].bitcast(E5M2X4), scales=scales[:], in_=v_bf[h][:].rearrange("p i t -> p (i t)")
+                )
+                for r in range(ROW_TILES):
+                    rows = slice(r * P, (r + 1) * P)
+                    nc.tensor.matmul_mx(
+                        out=acc[h][:, r, :],
+                        lhsT=u_codes[a][:, rows].bitcast(E5M2X4),
+                        lhsT_scale=u_scales[a][:, rows],
+                        rhs=codes[:].bitcast(E5M2X4),
+                        rhs_scale=scales[:],
+                        start=(a == 0 and r == 0),
+                        stop=(a == PASSES - 1 and r == ROW_TILES - 1),
+                    )
+
+        width = ROW_TILES * HALF
+        bundles = width // BUNDLE
+        score = [keep.tile([P, width], F32, name=f"score{h}") for h in range(HALVES)]
+        total = [keep.tile([P, bundles], F32, name=f"total{h}") for h in range(HALVES)]
+        size = [keep.tile([P, width], F32, name=f"size{h}") for h in range(HALVES)]
+        centred = [keep.tile([P, width], F32, name=f"centred{h}") for h in range(HALVES)]
+        result = [keep.tile([P, width], F32, name=f"result{h}") for h in range(HALVES)]
+        for h in range(HALVES):
+            nc.vector.tensor_tensor(
+                score[h][:].rearrange("p (r i) -> p r i", r=ROW_TILES),
+                acc[h][:],
+                bias[:, h * HALF : (h + 1) * HALF].unsqueeze(1).broadcast_to([P, ROW_TILES, HALF]),
+                ALU.add,
+            )
+            nc.scalar.activation(size[h][:], score[h][:], ACT.Abs)
+        for h in range(HALVES):
+            nc.vector.tensor_reduce(
+                total[h][:], score[h][:].rearrange("p (g e) -> p g e", e=BUNDLE), mybir.AxisListType.X, ALU.add
+            )
+        for h in range(HALVES):
+            nc.vector.scalar_tensor_tensor(
+                centred[h][:].rearrange("p (g e) -> p g e", e=BUNDLE),
+                total[h][:].unsqueeze(2).broadcast_to([P, bundles, BUNDLE]),
+                -1.0 / BUNDLE,
+                score[h][:].rearrange("p (g e) -> p g e", e=BUNDLE),
+                ALU.mult,
+                ALU.add,
+            )
+        for h in range(HALVES):
+            nc.vector.tensor_tensor(result[h][:], centred[h][:], size[h][:], ALU.mult)
+            nc.sync.dma_start(
+                out=out[:, h * HALF : (h + 1) * HALF].rearrange("(r p) i -> p r i", p=P),
+                in_=result[h][:].rearrange("p (r i) -> p r i", r=ROW_TILES),
+            )

@@ -48,12 +48,19 @@ def tile_list_scores_gaps_mixed_centred_f_kernel(tc, xf, fk, kf, ko, fi, bi, off
         fi_sb = keep.tile([P, PASSES, PACK], F32, name="fi_sb")
         bi_pairs = keep.tile([P, 2], F32, name="bi_pairs")
 
+        warm = keep.tile([P, 16], F32, name="warm")
+        nc.vector.memset(warm[:, 0:1], 0.0)
+        nc.scalar.activation(warm[:, 8:9], warm[:, 0:1], ACT.Abs)
         nc.sync.dma_start(out=x_pl[0][0][:], in_=xf_v[0, 0])
         nc.sync.dma_start(list2[:], offs2)
         nc.sync.dma_start(list1[:], offs)
         for n in range(1, PASSES * PACK):
             nc.sync.dma_start(out=x_pl[n // PACK][n % PACK][:], in_=xf_v[n // PACK, n % PACK])
+            if n == PACK - 1:
+                nc.sync.dma_start(out=fk_sb[:], in_=fk.rearrange("(a p t) o -> p a (t o)", a=PASSES, t=PACK))
         nc.sync.dma_start(list3[:], offs3)
+        nc.sync.dma_start(out=fi_sb[:], in_=fi.rearrange("(a p t) o -> p a (t o)", a=PASSES, t=PACK))
+        nc.sync.dma_start(out=bi_pairs[:], in_=bi.rearrange("o (p e) -> p (o e)", e=2))
         nc.sync.dma_start(out=ko_first[:], in_=ko_v[0])
         for t in range(PACK):
             nc.sync.dma_start(out=k_pl[0][t][:], in_=kf_v[0, t])
@@ -62,9 +69,6 @@ def tile_list_scores_gaps_mixed_centred_f_kernel(tc, xf, fk, kf, ko, fi, bi, off
             nc.sync.dma_start(out=k_pl[1][t][:], in_=kf_v[1, t])
         nc.sync.dma_start(out=ko_last[:], in_=ko_v[1, :, PACK - 1, :])
 
-        nc.gpsimd.dma_start(out=fk_sb[:], in_=fk.rearrange("(a p t) o -> p a (t o)", a=PASSES, t=PACK))
-        nc.gpsimd.dma_start(out=fi_sb[:], in_=fi.rearrange("(a p t) o -> p a (t o)", a=PASSES, t=PACK))
-        nc.gpsimd.dma_start(out=bi_pairs[:], in_=bi.rearrange("o (p e) -> p (o e)", e=2))
 
         ident = keep.tile([P, P], F32, name="ident")
         make_identity(nc, ident[:])
@@ -99,41 +103,45 @@ def tile_list_scores_gaps_mixed_centred_f_kernel(tc, xf, fk, kf, ko, fi, bi, off
 
         acc = [psum.tile([P, ROW_TILES, HALF], F32, name=f"acc{h}") for h in range(HALVES)]
         for a in range(PASSES):
-            v_bf = [keep.tile([P, HALF, PACK], BF16, name=f"v_bf{a}{h}", align_bytes=64) for h in range(HALVES)]
+            parts = [slice(0, I)] if a < PASSES - 1 else [slice(h * HALF, (h + 1) * HALF) for h in range(HALVES)]
+            v_bf = [
+                keep.tile([P, c.stop - c.start, PACK], BF16, name=f"v_bf{a}{n}", align_bytes=64)
+                for n, c in enumerate(parts)
+            ]
             for t in range(PACK):
+                last = a == PASSES - 1 and t == PACK - 1
                 if a == 0:
                     own = ko_first[:, t, :]
-                elif t < PACK - 1:
+                elif not last:
                     own = ko_most[:, t, :]
                 else:
                     own = ko_last[:]
-                sums = []
-                for h in range(HALVES):
-                    picked = ring.tile([P, HALF], F32, name="picked")
-                    part = list3[:, h * (HALF // 16) : (h + 1) * (HALF // 16)]
-                    nc.scalar.activation(picked[:], k_pl[a][t][:].indirect(part), ACT.Copy)
-                    key = ring.tile([P, HALF], F32, name="key")
-                    nc.vector.tensor_tensor(key[:], picked[:], own[:, h * HALF : (h + 1) * HALF], ALU.add)
-                    sums.append(key)
-                for h in range(HALVES):
-                    nc.vector.tensor_scalar(v_bf[h][:, :, t], sums[h][:], fi_sb[:, a, t : t + 1], None, ALU.mult)
-            for h in range(HALVES):
-                codes = keep.tile([P, HALF], U32, name=f"v_codes{a}{h}", align_bytes=64)
-                scales = keep.tile([P, HALF], U8, name=f"v_scales{a}{h}", align_bytes=64)
+                picked = ring.tile([P, I], F32, name="picked")
+                key = ring.tile([P, I], F32, name="key")
+                for c in parts if last else [slice(0, I)]:
+                    nc.scalar.activation(picked[:, c], k_pl[a][t][:].indirect(list3[:, c.start // 16 : c.stop // 16]), ACT.Copy)
+                    nc.vector.tensor_tensor(key[:, c], picked[:, c], own[:, c], ALU.add)
+                for n, c in enumerate(parts):
+                    nc.vector.tensor_scalar(v_bf[n][:, :, t], key[:, c], fi_sb[:, a, t : t + 1], None, ALU.mult)
+            for n, c in enumerate(parts):
+                codes = keep.tile([P, c.stop - c.start], U32, name=f"v_codes{a}{n}", align_bytes=64)
+                scales = keep.tile([P, c.stop - c.start], U8, name=f"v_scales{a}{n}", align_bytes=64)
                 nc.vector.quantize_mx(
-                    out=codes[:].bitcast(E5M2X4), scales=scales[:], in_=v_bf[h][:].rearrange("p i t -> p (i t)")
+                    out=codes[:].bitcast(E5M2X4), scales=scales[:], in_=v_bf[n][:].rearrange("p i t -> p (i t)")
                 )
-                for r in range(ROW_TILES):
-                    rows = slice(r * P, (r + 1) * P)
-                    nc.tensor.matmul_mx(
-                        out=acc[h][:, r, :],
-                        lhsT=u_codes[a][:, rows].bitcast(E5M2X4),
-                        lhsT_scale=u_scales[a][:, rows],
-                        rhs=codes[:].bitcast(E5M2X4),
-                        rhs_scale=scales[:],
-                        start=(a == 0 and r == 0),
-                        stop=(a == PASSES - 1 and r == ROW_TILES - 1),
-                    )
+                for h in range(c.start // HALF, c.stop // HALF):
+                    cols = slice(h * HALF - c.start, (h + 1) * HALF - c.start)
+                    for r in range(ROW_TILES):
+                        rows = slice(r * P, (r + 1) * P)
+                        nc.tensor.matmul_mx(
+                            out=acc[h][:, r, :],
+                            lhsT=u_codes[a][:, rows].bitcast(E5M2X4),
+                            lhsT_scale=u_scales[a][:, rows],
+                            rhs=codes[:, cols].bitcast(E5M2X4),
+                            rhs_scale=scales[:, cols],
+                            start=(a == 0 and r == 0),
+                            stop=(a == PASSES - 1 and r == ROW_TILES - 1),
+                        )
 
         width = ROW_TILES * HALF
         bundles = width // BUNDLE

@@ -33,7 +33,7 @@ def tile_list_scores_gaps_mixed_centred_f_kernel(tc, xf, fk, kf, ko, fi, bi, off
 
     with ExitStack() as ctx:
         keep = ctx.enter_context(tc.tile_pool(name="keep", bufs=1))
-        ring = ctx.enter_context(tc.tile_pool(name="ring", bufs=4))
+        ring = ctx.enter_context(tc.tile_pool(name="ring", bufs=PASSES * PACK))
         psum = ctx.enter_context(tc.psum_pool(name="psum", bufs=1))
 
         list1 = keep.tile([P, LIST_COLS], U16, name="list1")
@@ -48,19 +48,15 @@ def tile_list_scores_gaps_mixed_centred_f_kernel(tc, xf, fk, kf, ko, fi, bi, off
         fi_sb = keep.tile([P, PASSES, PACK], F32, name="fi_sb")
         bi_pairs = keep.tile([P, 2], F32, name="bi_pairs")
 
-        warm = keep.tile([P, 16], F32, name="warm")
-        nc.vector.memset(warm[:, 0:1], 0.0)
-        nc.scalar.activation(warm[:, 8:9], warm[:, 0:1], ACT.Abs)
+        nc.scalar.dma_start(out=bi_pairs[:], in_=bi.rearrange("o (p e) -> p (o e)", e=2))
+        nc.scalar.dma_start(out=fk_sb[:], in_=fk.rearrange("(a p t) o -> p a (t o)", a=PASSES, t=PACK))
+        nc.scalar.dma_start(out=fi_sb[:], in_=fi.rearrange("(a p t) o -> p a (t o)", a=PASSES, t=PACK))
         nc.sync.dma_start(out=x_pl[0][0][:], in_=xf_v[0, 0])
         nc.sync.dma_start(list2[:], offs2)
         nc.sync.dma_start(list1[:], offs)
         for n in range(1, PASSES * PACK):
             nc.sync.dma_start(out=x_pl[n // PACK][n % PACK][:], in_=xf_v[n // PACK, n % PACK])
-            if n == PACK - 1:
-                nc.sync.dma_start(out=fk_sb[:], in_=fk.rearrange("(a p t) o -> p a (t o)", a=PASSES, t=PACK))
         nc.sync.dma_start(list3[:], offs3)
-        nc.sync.dma_start(out=fi_sb[:], in_=fi.rearrange("(a p t) o -> p a (t o)", a=PASSES, t=PACK))
-        nc.sync.dma_start(out=bi_pairs[:], in_=bi.rearrange("o (p e) -> p (o e)", e=2))
         nc.sync.dma_start(out=ko_first[:], in_=ko_v[0])
         for t in range(PACK):
             nc.sync.dma_start(out=k_pl[0][t][:], in_=kf_v[0, t])
@@ -76,20 +72,22 @@ def tile_list_scores_gaps_mixed_centred_f_kernel(tc, xf, fk, kf, ko, fi, bi, off
         for e in range(2):
             nc.tensor.transpose(bias_ps[:, e, :], bi_pairs[:, e : e + 1].to_broadcast([P, P]), ident[:])
         bias = keep.tile([P, I], F32, name="bias")
+        nc.scalar.activation(
+            bias[:].rearrange("p (n e) -> p n e", e=2), bias_ps[:].rearrange("p e n -> p n e"), ACT.Copy
+        )
 
         u_codes, u_scales = [], []
         for a in range(PASSES):
-            gaps = keep.tile([P, PACK, J], F32, name=f"gaps{a}")
+            u_planes = keep.tile([P, PACK, J], BF16, name=f"u_planes{a}")
             for t in range(PACK):
                 second = ring.tile([P, J], F32, name="second")
+                gap = ring.tile([P, J], F32, name="gap")
                 nc.scalar.activation(second[:], x_pl[a][t][:].indirect(list2[:]), ACT.Copy)
-                nc.vector.tensor_tensor(gaps[:, t, :], x_pl[a][t][:].indirect(list1[:]), second[:], ALU.subtract)
+                nc.vector.tensor_tensor(gap[:], x_pl[a][t][:].indirect(list1[:]), second[:], ALU.subtract)
+                nc.vector.tensor_scalar(u_planes[:, t, :], gap[:], fk_sb[:, a, t : t + 1], None, ALU.mult)
             u_bf = keep.tile([P, J, PACK], BF16, name=f"u_bf{a}", align_bytes=64)
-            nc.vector.tensor_tensor(
-                u_bf[:].rearrange("p (c i) t -> p c t i", i=4),
-                gaps[:].rearrange("p t (c i) -> p c t i", i=4),
-                fk_sb[:, a, :].unsqueeze(1).unsqueeze(3).broadcast_to([P, J // 4, PACK, 4]),
-                ALU.mult,
+            nc.vector.tensor_copy(
+                u_bf[:].rearrange("p (c i) t -> p c t i", i=4), u_planes[:].rearrange("p t (c i) -> p c t i", i=4)
             )
             codes = keep.tile([P, J], U32, name=f"u_codes{a}", align_bytes=64)
             scales = keep.tile([P, J], U8, name=f"u_scales{a}", align_bytes=64)
@@ -99,8 +97,6 @@ def tile_list_scores_gaps_mixed_centred_f_kernel(tc, xf, fk, kf, ko, fi, bi, off
             u_codes.append(codes)
             u_scales.append(scales)
 
-        nc.scalar.copy(bias[:].rearrange("p (n e) -> p n e", e=2), bias_ps[:].rearrange("p e n -> p n e"))
-
         acc = [psum.tile([P, ROW_TILES, HALF], F32, name=f"acc{h}") for h in range(HALVES)]
         for a in range(PASSES):
             parts = [slice(0, I)] if a < PASSES - 1 else [slice(h * HALF, (h + 1) * HALF) for h in range(HALVES)]
@@ -108,6 +104,7 @@ def tile_list_scores_gaps_mixed_centred_f_kernel(tc, xf, fk, kf, ko, fi, bi, off
                 keep.tile([P, c.stop - c.start, PACK], BF16, name=f"v_bf{a}{n}", align_bytes=64)
                 for n, c in enumerate(parts)
             ]
+            v_planes = keep.tile([P, PACK, I], BF16, name="v_planes") if a < PASSES - 1 else None
             for t in range(PACK):
                 last = a == PASSES - 1 and t == PACK - 1
                 if a == 0:
@@ -121,8 +118,19 @@ def tile_list_scores_gaps_mixed_centred_f_kernel(tc, xf, fk, kf, ko, fi, bi, off
                 for c in parts if last else [slice(0, I)]:
                     nc.scalar.activation(picked[:, c], k_pl[a][t][:].indirect(list3[:, c.start // 16 : c.stop // 16]), ACT.Copy)
                     nc.vector.tensor_tensor(key[:, c], picked[:, c], own[:, c], ALU.add)
-                for n, c in enumerate(parts):
-                    nc.vector.tensor_scalar(v_bf[n][:, :, t], key[:, c], fi_sb[:, a, t : t + 1], None, ALU.mult)
+                    if a < PASSES - 1:
+                        nc.vector.tensor_scalar(v_planes[:, t, :], key[:], fi_sb[:, a, t : t + 1], None, ALU.mult)
+                        continue
+                    for n, d in enumerate(parts):
+                        if c.start <= d.start and d.stop <= c.stop:
+                            nc.vector.tensor_scalar(
+                                v_bf[n][:, :, t], key[:, d], fi_sb[:, a, t : t + 1], None, ALU.mult
+                            )
+            if a < PASSES - 1:
+                nc.vector.tensor_copy(
+                    v_bf[0][:].rearrange("p (c i) t -> p c t i", i=4),
+                    v_planes[:].rearrange("p t (c i) -> p c t i", i=4),
+                )
             for n, c in enumerate(parts):
                 codes = keep.tile([P, c.stop - c.start], U32, name=f"v_codes{a}{n}", align_bytes=64)
                 scales = keep.tile([P, c.stop - c.start], U8, name=f"v_scales{a}{n}", align_bytes=64)

from contextlib import ExitStack

import concourse.mybir as mybir
from concourse.masks import make_identity

K, T, J, I, V = 1024, 1024, 256, 256, 1024
BUNDLE = 8
FLOPS = 2 * K * J * I

F32 = mybir.dt.float32
BF16 = mybir.dt.bfloat16
U32 = mybir.dt.uint32
U16 = mybir.dt.uint16
U8 = mybir.dt.uint8
E5M2X4 = mybir.dt.float8_e5m2_x4
ALU = mybir.AluOpType
ACT = mybir.ActivationFunctionType

P = 128
PACK = 4
PASSES = K // (P * PACK)
HALF = 128
HALVES = I // HALF
ROW_TILES = J // P
LIST_COLS = J // 16


def tile_list_scores_gaps_mixed_centred_f_kernel(tc, xf, fk, kf, ko, fi, bi, offs, offs2, offs3, out):
    nc = tc.nc
    xf_v = xf.rearrange("(a p t) c -> a t p c", a=PASSES, t=PACK)
    kf_v = kf.rearrange("(a p t) c -> a t p c", a=PASSES, t=PACK)
    ko_v = ko.rearrange("(a p t) c -> a p t c", a=PASSES, t=PACK)

    with ExitStack() as ctx:
        keep = ctx.enter_context(tc.tile_pool(name="keep", bufs=1))
        ring = ctx.enter_context(tc.tile_pool(name="ring", bufs=PASSES * PACK))
        psum = ctx.enter_context(tc.psum_pool(name="psum", bufs=1))

        list1 = keep.tile([P, LIST_COLS], U16, name="list1")
        list2 = keep.tile([P, LIST_COLS], U16, name="list2")
        list3 = keep.tile([P, LIST_COLS], U16, name="list3")
        x_pl = [[keep.tile([P, T], F32, name=f"x{a}{t}") for t in range(PACK)] for a in range(PASSES)]
        k_pl = [[keep.tile([P, V], F32, name=f"k{a}{t}") for t in range(PACK)] for a in range(PASSES)]
        ko_first = keep.tile([P, PACK, I], F32, name="ko_first")
        ko_most = keep.tile([P, PACK - 1, I], F32, name="ko_most")
        ko_last = keep.tile([P, I], F32, name="ko_last")
        fk_sb = keep.tile([P, PASSES, PACK], F32, name="fk_sb")
        fi_sb = keep.tile([P, PASSES, PACK], F32, name="fi_sb")
        bi_pairs = keep.tile([P, 2], F32, name="bi_pairs")

        nc.scalar.dma_start(out=bi_pairs[:], in_=bi.rearrange("o (p e) -> p (o e)", e=2))
        nc.scalar.dma_start(out=fk_sb[:], in_=fk.rearrange("(a p t) o -> p a (t o)", a=PASSES, t=PACK))
        nc.scalar.dma_start(out=fi_sb[:], in_=fi.rearrange("(a p t) o -> p a (t o)", a=PASSES, t=PACK))
        nc.sync.dma_start(out=x_pl[0][0][:], in_=xf_v[0, 0])
        nc.sync.dma_start(list2[:], offs2)
        nc.sync.dma_start(list1[:], offs)
        for n in range(1, PASSES * PACK):
            nc.sync.dma_start(out=x_pl[n // PACK][n % PACK][:], in_=xf_v[n // PACK, n % PACK])
        nc.sync.dma_start(list3[:], offs3)
        nc.sync.dma_start(out=ko_first[:], in_=ko_v[0])
        for t in range(PACK):
            nc.sync.dma_start(out=k_pl[0][t][:], in_=kf_v[0, t])
        nc.sync.dma_start(out=ko_most[:], in_=ko_v[1, :, 0 : PACK - 1, :])
        for t in range(PACK):
            nc.sync.dma_start(out=k_pl[1][t][:], in_=kf_v[1, t])
        nc.sync.dma_start(out=ko_last[:], in_=ko_v[1, :, PACK - 1, :])


        ident = keep.tile([P, P], F32, name="ident")
        make_identity(nc, ident[:])
        bias_ps = psum.tile([P, 2, P], F32, name="bias_ps")
        for e in range(2):
            nc.tensor.transpose(bias_ps[:, e, :], bi_pairs[:, e : e + 1].to_broadcast([P, P]), ident[:])
        bias = keep.tile([P, I], F32, name="bias")
        nc.scalar.activation(
            bias[:].rearrange("p (n e) -> p n e", e=2), bias_ps[:].rearrange("p e n -> p n e"), ACT.Copy
        )

        u_codes, u_scales = [], []
        for a in range(PASSES):
            u_planes = keep.tile([P, PACK, J], BF16, name=f"u_planes{a}")
            for t in range(PACK):
                second = ring.tile([P, J], F32, name="second")
                gap = ring.tile([P, J], F32, name="gap")
                nc.scalar.activation(second[:], x_pl[a][t][:].indirect(list2[:]), ACT.Copy)
                nc.vector.tensor_tensor(gap[:], x_pl[a][t][:].indirect(list1[:]), second[:], ALU.subtract)
                nc.vector.tensor_scalar(u_planes[:, t, :], gap[:], fk_sb[:, a, t : t + 1], None, ALU.mult)
            u_bf = keep.tile([P, J, PACK], BF16, name=f"u_bf{a}", align_bytes=64)
            nc.vector.tensor_copy(
                u_bf[:].rearrange("p (c i) t -> p c t i", i=4), u_planes[:].rearrange("p t (c i) -> p c t i", i=4)
            )
            codes = keep.tile([P, J], U32, name=f"u_codes{a}", align_bytes=64)
            scales = keep.tile([P, J], U8, name=f"u_scales{a}", align_bytes=64)
            nc.vector.quantize_mx(
                out=codes[:].bitcast(E5M2X4), scales=scales[:], in_=u_bf[:].rearrange("p j t -> p (j t)")
            )
            u_codes.append(codes)
            u_scales.append(scales)

        acc = [psum.tile([P, ROW_TILES, HALF], F32, name=f"acc{h}") for h in range(HALVES)]
        for a in range(PASSES):
            parts = [slice(0, I)] if a < PASSES - 1 else [slice(h * HALF, (h + 1) * HALF) for h in range(HALVES)]
            v_bf = [
                keep.tile([P, c.stop - c.start, PACK], BF16, name=f"v_bf{a}{n}", align_bytes=64)
                for n, c in enumerate(parts)
            ]
            v_planes = keep.tile([P, PACK, I], BF16, name="v_planes") if a < PASSES - 1 else None
            for t in range(PACK):
                last = a == PASSES - 1 and t == PACK - 1
                if a == 0:
                    own = ko_first[:, t, :]
                elif not last:
                    own = ko_most[:, t, :]
                else:
                    own = ko_last[:]
                picked = ring.tile([P, I], F32, name="picked")
                key = ring.tile([P, I], F32, name="key")
                for c in parts if last else [slice(0, I)]:
                    nc.scalar.activation(picked[:, c], k_pl[a][t][:].indirect(list3[:, c.start // 16 : c.stop // 16]), ACT.Copy)
                    nc.vector.tensor_tensor(key[:, c], picked[:, c], own[:, c], ALU.add)
                    if a < PASSES - 1:
                        nc.vector.tensor_scalar(v_planes[:, t, :], key[:], fi_sb[:, a, t : t + 1], None, ALU.mult)
                        continue
                    for n, d in enumerate(parts):
                        if c.start <= d.start and d.stop <= c.stop:
                            nc.vector.tensor_scalar(
                                v_bf[n][:, :, t], key[:, d], fi_sb[:, a, t : t + 1], None, ALU.mult
                            )
            if a < PASSES - 1:
                nc.vector.tensor_copy(
                    v_bf[0][:].rearrange("p (c i) t -> p c t i", i=4),
                    v_planes[:].rearrange("p t (c i) -> p c t i", i=4),
                )
            for n, c in enumerate(parts):
                codes = keep.tile([P, c.stop - c.start], U32, name=f"v_codes{a}{n}", align_bytes=64)
                scales = keep.tile([P, c.stop - c.start], U8, name=f"v_scales{a}{n}", align_bytes=64)
                nc.vector.quantize_mx(
                    out=codes[:].bitcast(E5M2X4), scales=scales[:], in_=v_bf[n][:].rearrange("p i t -> p (i t)")
                )
                for h in range(c.start // HALF, c.stop // HALF):
                    cols = slice(h * HALF - c.start, (h + 1) * HALF - c.start)
                    for r in range(ROW_TILES):
                        rows = slice(r * P, (r + 1) * P)
                        nc.tensor.matmul_mx(
                            out=acc[h][:, r, :],
                            lhsT=u_codes[a][:, rows].bitcast(E5M2X4),
                            lhsT_scale=u_scales[a][:, rows],
                            rhs=codes[:, cols].bitcast(E5M2X4),
                            rhs_scale=scales[:, cols],
                            start=(a == 0 and r == 0),
                            stop=(a == PASSES - 1 and r == ROW_TILES - 1),
                        )

        width = ROW_TILES * HALF
        bundles = width // BUNDLE
        score = [keep.tile([P, width], F32, name=f"score{h}") for h in range(HALVES)]
        total = [keep.tile([P, bundles], F32, name=f"total{h}") for h in range(HALVES)]
        size = [keep.tile([P, width], F32, name=f"size{h}") for h in range(HALVES)]
        centred = [keep.tile([P, width], F32, name=f"centred{h}") for h in range(HALVES)]
        result = [keep.tile([P, width], F32, name=f"result{h}") for h in range(HALVES)]
        for h in range(HALVES):
            nc.vector.tensor_tensor(
                score[h][:].rearrange("p (r i) -> p r i", r=ROW_TILES),
                acc[h][:],
                bias[:, h * HALF : (h + 1) * HALF].unsqueeze(1).broadcast_to([P, ROW_TILES, HALF]),
                ALU.add,
            )
            nc.scalar.activation(size[h][:], score[h][:], ACT.Abs)
        for h in range(HALVES):
            nc.vector.tensor_reduce(
                total[h][:], score[h][:].rearrange("p (g e) -> p g e", e=BUNDLE), mybir.AxisListType.X, ALU.add
            )
        for h in range(HALVES):
            nc.vector.scalar_tensor_tensor(
                centred[h][:].rearrange("p (g e) -> p g e", e=BUNDLE),
                total[h][:].unsqueeze(2).broadcast_to([P, bundles, BUNDLE]),
                -1.0 / BUNDLE,
                score[h][:].rearrange("p (g e) -> p g e", e=BUNDLE),
                ALU.mult,
                ALU.add,
            )
        for h in range(HALVES):
            nc.vector.tensor_tensor(result[h][:], centred[h][:], size[h][:], ALU.mult)
            nc.sync.dma_start(
                out=out[:, h * HALF : (h + 1) * HALF].rearrange("(r p) i -> p r i", p=P),
                in_=result[h][:].rearrange("p (r i) -> p r i", r=ROW_TILES),
            )
